import numpy as np
import ml_dtypes


def mxq(x, axis, fmt="e4m3"):
    dtype, down = {"e4m3": (ml_dtypes.float8_e4m3fn, 7), "e5m2": (ml_dtypes.float8_e5m2, 14)}[fmt]
    v = np.moveaxis(np.asarray(x, np.float32).astype(ml_dtypes.bfloat16).astype(np.float64), axis, -1)
    blocks = v.reshape(v.shape[:-1] + (-1, 32))
    amax = np.abs(blocks).max(-1, keepdims=True)
    byte = np.maximum(np.where(amax > 0, np.frexp(amax)[1] - 1 + 127, 0) - down, 1)
    scale = np.exp2(byte - 127.0)
    codes = (blocks / scale).astype(np.float32).astype(dtype).astype(np.float64)
    return np.moveaxis((codes * scale).reshape(v.shape), -1, axis)


WIDE = False


def mx_kscale(k):
    if not WIDE:
        return np.ones(k)
    levels = np.array([10, -10, 5, -5, 0])
    if k % 512:
        return np.exp2(np.random.permutation(np.resize(levels, k // 32))).repeat(32)
    a = np.empty((k // 512, 16))
    for p in range(k // 512):
        a[p, :8] = np.random.permutation(np.resize(levels, 8))
        for g in range(8):
            far = levels[np.abs(levels - a[p, g]) >= 10]
            a[p, g + 8] = far[np.random.randint(len(far))]
    return np.exp2(a.ravel()).repeat(32)


def f64(x):
    return np.asarray(x).astype(np.float64)


def striped(idx):
    return np.tile(np.asarray(idx).reshape(-1, 16).T, (8, 1)).astype(np.uint16)


def unstriped(offs):
    return offs[:16].T.reshape(-1).astype(np.int64)


E2M1 = np.array([0.0, 0.5, 1.0, 1.5, 2.0, 3.0, 4.0, 6.0, -0.0, -0.5, -1.0, -1.5, -2.0, -3.0, -4.0, -6.0])


def pack_weight(w, fmt):
    k, n = w.shape
    w = f64(np.asarray(w, np.float32).astype(ml_dtypes.bfloat16)).reshape(k // 32, 32, n)
    amax = np.abs(w).max(1)
    if fmt == "e4m3":
        byte = np.frexp(amax)[1] - 1 + 127 - 7
    else:
        mant, ex = np.frexp(amax / 6.0)
        byte = np.where(mant > 0.5, ex, ex - 1) + 127
    byte = np.clip(np.where(amax > 0, byte, 1), 1, 254)
    scaled = (w * np.exp2(127.0 - byte)[:, None, :]).reshape(k, n).astype(np.float32)
    by_word = np.ascontiguousarray(scaled.reshape(k // 512, 128, 4, n).transpose(0, 1, 3, 2))
    if fmt == "e4m3":
        words = by_word.astype(ml_dtypes.float8_e4m3fn).view(np.uint8)
    else:
        c = by_word.astype(ml_dtypes.float4_e2m1fn).view(np.uint8) & 0xF
        words = (c[..., 0::2] | (c[..., 1::2] << 4)).reshape(k // 512, 128, 2 * n)
    return np.ascontiguousarray(words), np.ascontiguousarray(byte.astype(np.uint8).reshape(k // 512, 16, n))


def unpack_weight(words, scales, fmt):
    g, _, n = scales.shape
    words = np.ascontiguousarray(words).reshape(g, 128, n, -1)
    if fmt == "e4m3":
        vals = words.view(ml_dtypes.float8_e4m3fn).astype(np.float64)
    else:
        nib = np.empty((g, 128, n, 4), np.uint8)
        nib[..., 0::2] = words & 0xF
        nib[..., 1::2] = words >> 4
        vals = E2M1[nib]
    vals = vals * np.repeat(np.exp2(scales.astype(np.float64) - 127.0), 8, axis=1)[..., None]
    return vals.transpose(0, 1, 3, 2).reshape(g * 512, n)


def sigmoid(v):
    return 1.0 / (1.0 + np.exp(-v))


D, K, R, T, I, Q, G = 512, 512, 512, 2048, 512, 128, 32


def setup_inputs():
    n = np.random.standard_normal
    idx = np.random.permutation(T)[:I]
    fd = mx_kscale(D)
    fk = mx_kscale(K)
    fr = mx_kscale(R)
    keysp = pack_weight(n((D, T)) / fd[:, None], "e2m1")
    tabp = pack_weight(n((K, T)) / fk[:, None], "e2m1")
    return {
        "query": (n((D, Q)) * 0.6 / np.sqrt(D) * fd[:, None]).astype(np.float32),
        "query2": (n((D, Q)) * 1.0 / np.sqrt(D) * fd[:, None]).astype(np.float32),
        "keys_words": keysp[0],
        "keys_scales": keysp[1],
        "tab_words": tabp[0],
        "tab_scales": tabp[1],
        "w1": (n((K, R)) * 1 / np.sqrt(K) * fk[:, None]).astype(np.float32),
        "share": (np.random.uniform(0.4, 1.0, (R, 1))).astype(np.float32),
        "gout": (n((R, Q)) * 1 / np.sqrt(R) * fr[:, None]).astype(np.float32),
        "hsc": (np.random.uniform(0.7, 1.4, (R, 1)) / fr[:, None]).astype(np.float32),
        "old": (0.5 * n((Q, T))).astype(np.float32),
        "offs": striped(idx),
    }


def reference(query, query2, keys_words, keys_scales, tab_words, tab_scales, w1, share, gout, hsc, old, offs):
    idx = unstriped(offs)
    keysu = unpack_weight(keys_words, keys_scales, "e2m1")
    tabu = unpack_weight(tab_words, tab_scales, "e2m1")
    queryq = mxq(f64(query), 0, "e4m3")
    keysidxg = keysu[:, idx]
    a = queryq.T @ keysidxg
    query2q = mxq(f64(query2), 0, "e4m3")
    b = query2q.T @ keysidxg
    p = np.exp(a - np.max(a, axis=1, keepdims=True)) * sigmoid(b)
    z = np.sum(p, axis=1, keepdims=True)
    w1q = mxq(f64(w1), 0, "e4m3")
    tabidxg = tabu[:, idx]
    zh = w1q.T @ tabidxg
    mz = zh.reshape(R, G, I // G).mean(axis=2)
    mzr = np.repeat(mz, I // G, axis=1)
    hv = np.tanh(zh - mzr * f64(share))
    hs1 = hv * f64(hsc)
    goutq = mxq(f64(gout), 0, "e4m3")
    hs1q = mxq(hs1, 0, "e4m3")
    c0 = goutq.T @ hs1q
    dz = np.sum(c0 * p / np.square(z) * (-1.0), axis=1, keepdims=True)
    dp = c0 / z + dz
    da = dp * sigmoid(b) * np.exp(a - np.max(a, axis=1, keepdims=True))
    gs = da * 512.0
    gf = np.zeros((Q, T))
    gf[:, idx] = gs
    y = f64(old) + gf
    return y

@@ -1,0 +1,220 @@
+from contextlib import ExitStack
+
+import concourse.mybir as mybir
+
+D, K, R, T, I, Q, G = 512, 512, 512, 2048, 512, 128, 32
+FLOPS = 2 * I * (2 * D * Q + K * R + R * Q)
+
+F32 = mybir.dt.float32
+BF16 = mybir.dt.bfloat16
+I32 = mybir.dt.int32
+U32 = mybir.dt.uint32
+U16 = mybir.dt.uint16
+U8 = mybir.dt.uint8
+FP8X4 = mybir.dt.float8_e4m3fn_x4
+FP4X4 = mybir.dt.float4_e2m1fn_x4
+ALU = mybir.AluOpType
+ACT = mybir.ActivationFunctionType
+AX = mybir.AxisListType
+
+P = 128
+PACK = 4
+PAGE = I // G
+CHUNK = 128
+CHUNKS = I // CHUNK
+PAGES = CHUNK // PAGE
+HALVES = 2
+OUT_PARTS = 4
+
+
+def tile_attend_blrcentred_asked_kernel(tc, query, query2, keys_words, keys_scales, tab_words, tab_scales,
+                                         w1, share, gout, hsc, old, offs, out):
+    nc = tc.nc
+    with ExitStack() as ctx:
+        keep = ctx.enter_context(tc.tile_pool(name="keep", bufs=1))
+        psum = ctx.enter_context(tc.psum_pool(name="psum", bufs=1))
+
+        def tile(shape, dtype, name, tag=None):
+            return keep.tile(shape, dtype, name=name, tag=tag or name, align_bytes=64)
+
+        offsets = keep.tile([P, I // 16], U16, name="offsets")
+        nc.sync.dma_start(offsets[:], offs)
+
+        key_bytes = tile([P, T], U8, "key_bytes")
+        tab_bytes = tile([P, T], U8, "tab_bytes")
+        nc.vector.memset(key_bytes[:].bitcast(I32), 0)
+        nc.vector.memset(tab_bytes[:].bitcast(I32), 0)
+        warm = tile([P, 2], F32, "warm")
+        nc.vector.memset(warm[:, 0:1], 0.0)
+        placed = tile([P, T], F32, "placed")
+        nc.vector.memset(placed[:], 0.0)
+
+        def load_scale_rows(queue, window, scales, quads):
+            for quad in quads:
+                queue.dma_start(window[32 * quad : 32 * quad + 4, :].bitcast(I32),
+                                scales[0, 4 * quad : 4 * quad + 4, :].bitcast(I32))
+
+        def load_rows(source, name, tag):
+            rows = tile([P, PACK, source.shape[1]], F32, name, tag)
+            nc.sync.dma_start(rows[:], source.rearrange("(p j) c -> p j c", j=PACK))
+            return rows
+
+        def load_words(source, name, tag):
+            words = tile([P, T], U16, name, tag)
+            nc.sync.dma_start(words[:].bitcast(I32), source[0].bitcast(I32))
+            return words
+
+        half = R // HALVES
+        load_scale_rows(nc.scalar, key_bytes, keys_scales, range(4))
+        load_scale_rows(nc.gpsimd, tab_bytes, tab_scales, (2, 3))
+        nc.scalar.activation(warm[:, 1:2], warm[:, 0:1], ACT.Sigmoid)
+        key_pool = load_words(keys_words, "key_pool", "key_pool")
+        q2_raw = load_rows(query2, "q2_raw", "stage_b")
+        w_lo = load_rows(w1[:, 0:half], "w_lo", "stage_d")
+        tab_pool = load_words(tab_words, "tab_pool", "stage_c")
+        w_hi = load_rows(w1[:, half:R], "w_hi", "w_hi")
+        share_sb = tile([P, PACK], F32, "share_sb")
+        hsc_sb = tile([P, PACK], F32, "hsc_sb")
+        nc.gpsimd.dma_start(share_sb[:], share.rearrange("(p t) o -> p (t o)", t=PACK))
+        nc.gpsimd.dma_start(hsc_sb[:], hsc.rearrange("(p t) o -> p (t o)", t=PACK))
+        part = T // OUT_PARTS
+
+        def gather(window, dtype, name):
+            picked = tile([P, I], dtype, name)
+            nc.vector.tensor_copy(picked[:], window[:].indirect(offsets[:]))
+            return picked
+
+        def quantise(grouped, columns, name):
+            codes = tile([P, columns], U32, f"{name}_codes")
+            plane = tile([P, columns], U8, f"{name}_plane")
+            nc.vector.quantize_mx(out=codes[:].bitcast(FP8X4), scales=plane[:], in_=grouped)
+            return codes, plane
+
+        def interleave(copy, rows, name):
+            grouped = tile([P, Q * PACK], BF16, name)
+            copy(grouped[:].rearrange("p (c i j) -> p c j i", i=4, j=PACK), rows[:].rearrange("p j (c i) -> p c j i", i=4))
+            return grouped
+
+        def score(operand, name):
+            bank = psum.tile([P, I], F32, name=name)
+            nc.tensor.matmul_mx(out=bank[:], lhsT=operand[0][:].bitcast(FP8X4), lhsT_scale=operand[1][:],
+                                rhs=key_codes[:].bitcast(FP4X4), rhs_scale=key_plane[:], start=True, stop=True)
+            return bank
+
+        key_codes = gather(key_pool, U16, "key_codes")
+        q2_grouped = interleave(nc.scalar.copy, q2_raw, "q2_grouped")
+        load_scale_rows(nc.scalar, tab_bytes, tab_scales, (0, 1))
+        q_raw = load_rows(query, "q_raw", "stage_b")
+        q2_operand = quantise(q2_grouped[:], Q, "q2")
+        key_plane = gather(key_bytes, U8, "key_plane")
+        b_scores = score(q2_operand, "b_scores")
+        tab_codes = gather(tab_pool, U16, "tab_codes")
+        tab_plane = gather(tab_bytes, U8, "tab_plane")
+
+        w_grouped = tile([P, PACK * P * PACK], BF16, "w_grouped")
+        w_dealt = w_grouped[:].rearrange("p (t m j) -> p m j t", t=PACK, j=PACK)
+        span = half // PACK
+        nc.scalar.copy(w_dealt[:, 0:span], w_lo[:].rearrange("p j (m t) -> p m j t", t=PACK))
+        g_raw = load_rows(gout, "g_raw", "stage_d")
+        old_sb = tile([P, T], F32, "old_sb", "stage_c")
+        nc.sync.dma_start(old_sb[:], old)
+        gate = tile([P, I], F32, "gate")
+        nc.scalar.activation(gate[:], b_scores[:], ACT.Sigmoid)
+        nc.scalar.copy(w_dealt[:, span:P], w_hi[:].rearrange("p j (m t) -> p m j t", t=PACK))
+        warm_exp = tile([P, 1], F32, "warm_exp")
+        nc.scalar.activation(warm_exp[:], w_grouped[:, PACK * span : PACK * span + 1], ACT.Exp, scale=0.0, bias=gate[:, 0:1])
+        a_scores = score(quantise(interleave(nc.vector.tensor_copy, q_raw, "q_grouped")[:], Q, "q"), "a_scores")
+        w_codes, w_plane = quantise(w_grouped[:], R, "w")
+
+        zh = [psum.tile([P, PACK, CHUNK], F32, name=f"zh{c}") for c in range(CHUNKS)]
+        for c in range(CHUNKS):
+            cols = slice(c * CHUNK, (c + 1) * CHUNK)
+            for t in range(PACK):
+                rows = slice(t * P, (t + 1) * P)
+                nc.tensor.matmul_mx(out=zh[c][:, t, :], lhsT=w_codes[:, rows].bitcast(FP8X4), lhsT_scale=w_plane[:, rows],
+                                    rhs=tab_codes[:, cols].bitcast(FP4X4), rhs_scale=tab_plane[:, cols],
+                                    start=True, stop=True)
+
+        share_mean = tile([P, PACK], F32, "share_mean")
+        nc.gpsimd.tensor_scalar(share_mean[:], share_sb[:], 1.0 / PAGE, 0.0, ALU.mult, ALU.add)
+
+        sums = [tile([P, PACK, 2 * PAGES], F32, f"sums{pair}") for pair in range(CHUNKS // 2)]
+        centre = [tile([P, PACK, 2 * PAGES], F32, f"centre{pair}") for pair in range(CHUNKS // 2)]
+        hv = [tile([P, CHUNK * PACK], F32, f"hv{c}") for c in range(CHUNKS)]
+        hs = [tile([P, CHUNK * PACK], BF16, f"hs{c}") for c in range(CHUNKS)]
+
+        def own_pages(c):
+            return slice((c % 2) * PAGES, (c % 2 + 1) * PAGES)
+
+        def page_sums(c):
+            nc.vector.tensor_reduce(sums[c // 2][:, :, own_pages(c)], zh[c][:].rearrange("p t (g j) -> p t g j", j=PAGE),
+                                    AX.X, ALU.add)
+
+        def page_centres(pair):
+            for t in range(PACK):
+                nc.scalar.activation(centre[pair][:, t, :], sums[pair][:, t, :], ACT.Copy, scale=share_mean[:, t : t + 1])
+
+        def squash(c):
+            centred = tile([P, CHUNK * PACK], F32, f"centred{c}")
+            spread = centre[c // 2][:, :, own_pages(c)].rearrange("p t g -> p g t").unsqueeze(2)
+            nc.vector.tensor_tensor(centred[:].rearrange("p (g j t) -> p g j t", j=PAGE, t=PACK),
+                                    zh[c][:].rearrange("p t (g j) -> p g j t", j=PAGE),
+                                    spread.broadcast_to([P, PAGES, PAGE, PACK]), ALU.subtract)
+            nc.scalar.activation(hv[c][:], centred[:], ACT.Tanh)
+
+        def scale(engine, c):
+            engine.tensor_tensor(hs[c][:].rearrange("p (i t) -> p i t", t=PACK), hv[c][:].rearrange("p (i t) -> p i t", t=PACK),
+                                 hsc_sb[:].unsqueeze(1).broadcast_to([P, CHUNK, PACK]), ALU.mult)
+
+        def project(c):
+            h_codes, h_plane = quantise(hs[c][:], CHUNK, f"hs{c}")
+            nc.tensor.matmul_mx(out=c0[:, c * CHUNK : (c + 1) * CHUNK], lhsT=g_codes[:].bitcast(FP8X4), lhsT_scale=g_plane[:],
+                                rhs=h_codes[:].bitcast(FP8X4), rhs_scale=h_plane[:], start=True, stop=True)
+
+        neg_max = tile([P, 1], F32, "neg_max")
+        nc.vector.tensor_reduce(neg_max[:], a_scores[:], AX.X, ALU.max, negate=True)
+        expo = tile([P, I], F32, "expo")
+        nc.scalar.activation(expo[:], a_scores[:], ACT.Exp, bias=neg_max[:])
+        p = tile([P, I], F32, "p")
+        nc.gpsimd.tensor_tensor(p[:], expo[:], gate[:], ALU.mult)
+        page_sums(0)
+        page_sums(1)
+        page_centres(0)
+        page_sums(2)
+        squash(0)
+        scale(nc.gpsimd, 0)
+        page_sums(3)
+        page_centres(1)
+        for c in range(1, CHUNKS):
+            squash(c)
+        g_grouped = interleave(nc.scalar.copy, g_raw, "g_grouped")
+        z = tile([P, 1], F32, "z")
+        nc.scalar.activation(expo[:], p[:], ACT.Copy, accum_out=z[:])
+        g_codes, g_plane = quantise(g_grouped[:], Q, "g")
+        c0 = psum.tile([P, I], F32, name="c0")
+        scale(nc.vector, 1)
+        project(0)
+        scale(nc.vector, 2)
+        project(1)
+        scale(nc.vector, 3)
+        project(2)
+        rz = tile([P, 1], F32, "rz")
+        nc.vector.reciprocal(rz[:], z[:])
+        project(3)
+        gain = tile([P, 1], F32, "gain")
+        nc.vector.tensor_scalar(gain[:], rz[:], 512.0, None, ALU.mult)
+        neg_rz = tile([P, 1], F32, "neg_rz")
+        nc.vector.tensor_scalar(neg_rz[:], rz[:], -1.0, None, ALU.mult)
+
+        cp = tile([P, I], F32, "cp")
+        total = tile([P, 1], F32, "total")
+        nc.vector.scalar_tensor_tensor(cp[:], c0[:], gain[:], p[:], ALU.mult, ALU.mult, accum_out=total[:])
+        u = tile([P, I], F32, "u")
+        nc.vector.tensor_scalar(u[:], p[:], total[:], neg_rz[:], ALU.mult, ALU.mult)
+        nc.vector.tensor_tensor(placed[:].indirect(offsets[:]), cp[:], u[:], ALU.add)
+
+        for s in range(OUT_PARTS):
+            cols = slice(s * part, (s + 1) * part)
+            res = tile([P, part], F32, f"res{s}")
+            nc.vector.tensor_tensor(res[:], placed[:, cols], old_sb[:, cols], ALU.add)
+            nc.sync.dma_start(out[:, cols], res[:])

@@ -65,18 +65,22 @@ def tile_attend_blrcentred_asked_kernel(tc, query, query2, keys_words, keys_scal
             return words
 
         half = R // HALVES
-        load_scale_rows(nc.scalar, key_bytes, keys_scales, range(4))
-        load_scale_rows(nc.gpsimd, tab_bytes, tab_scales, (2, 3))
         nc.scalar.activation(warm[:, 1:2], warm[:, 0:1], ACT.Sigmoid)
         key_pool = load_words(keys_words, "key_pool", "key_pool")
-        q2_raw = load_rows(query2, "q2_raw", "stage_b")
-        w_lo = load_rows(w1[:, 0:half], "w_lo", "stage_d")
-        tab_pool = load_words(tab_words, "tab_pool", "stage_c")
+        load_scale_rows(nc.sync, key_bytes, keys_scales, range(4))
+        q2_raw = load_rows(query2, "q2_raw", "q2_raw")
+        w_lo = load_rows(w1[:, 0:half], "w_lo", "w_lo")
+        load_scale_rows(nc.sync, tab_bytes, tab_scales, range(4))
+        tab_pool = load_words(tab_words, "tab_pool", "tab_pool")
         w_hi = load_rows(w1[:, half:R], "w_hi", "w_hi")
+        q_raw = load_rows(query, "q_raw", "q_raw")
         share_sb = tile([P, PACK], F32, "share_sb")
+        nc.sync.dma_start(share_sb[:], share.rearrange("(p t) o -> p (t o)", t=PACK))
+        g_raw = load_rows(gout, "g_raw", "g_raw")
         hsc_sb = tile([P, PACK], F32, "hsc_sb")
-        nc.gpsimd.dma_start(share_sb[:], share.rearrange("(p t) o -> p (t o)", t=PACK))
-        nc.gpsimd.dma_start(hsc_sb[:], hsc.rearrange("(p t) o -> p (t o)", t=PACK))
+        nc.sync.dma_start(hsc_sb[:], hsc.rearrange("(p t) o -> p (t o)", t=PACK))
+        old_sb = tile([P, T], F32, "old_sb")
+        nc.sync.dma_start(old_sb[:], old)
         part = T // OUT_PARTS
 
         def gather(window, dtype, name):
@@ -103,21 +107,16 @@ def tile_attend_blrcentred_asked_kernel(tc, query, query2, keys_words, keys_scal
 
         key_codes = gather(key_pool, U16, "key_codes")
         q2_grouped = interleave(nc.scalar.copy, q2_raw, "q2_grouped")
-        load_scale_rows(nc.scalar, tab_bytes, tab_scales, (0, 1))
-        q_raw = load_rows(query, "q_raw", "stage_b")
-        q2_operand = quantise(q2_grouped[:], Q, "q2")
         key_plane = gather(key_bytes, U8, "key_plane")
+        q2_operand = quantise(q2_grouped[:], Q, "q2")
         b_scores = score(q2_operand, "b_scores")
-        tab_codes = gather(tab_pool, U16, "tab_codes")
         tab_plane = gather(tab_bytes, U8, "tab_plane")
+        tab_codes = gather(tab_pool, U16, "tab_codes")
 
         w_grouped = tile([P, PACK * P * PACK], BF16, "w_grouped")
         w_dealt = w_grouped[:].rearrange("p (t m j) -> p m j t", t=PACK, j=PACK)
         span = half // PACK
         nc.scalar.copy(w_dealt[:, 0:span], w_lo[:].rearrange("p j (m t) -> p m j t", t=PACK))
-        g_raw = load_rows(gout, "g_raw", "stage_d")
-        old_sb = tile([P, T], F32, "old_sb", "stage_c")
-        nc.sync.dma_start(old_sb[:], old)
         gate = tile([P, I], F32, "gate")
         nc.scalar.activation(gate[:], b_scores[:], ACT.Sigmoid)
         nc.scalar.copy(w_dealt[:, span:P], w_hi[:].rearrange("p j (m t) -> p m j t", t=PACK))
@@ -136,10 +135,10 @@ def tile_attend_blrcentred_asked_kernel(tc, query, query2, keys_words, keys_scal
                                     start=True, stop=True)
 
         share_mean = tile([P, PACK], F32, "share_mean")
-        nc.gpsimd.tensor_scalar(share_mean[:], share_sb[:], 1.0 / PAGE, 0.0, ALU.mult, ALU.add)
+        nc.scalar.activation(share_mean[:], share_sb[:], ACT.Copy, scale=1.0 / PAGE)
 
         sums = [tile([P, PACK, 2 * PAGES], F32, f"sums{pair}") for pair in range(CHUNKS // 2)]
-        centre = [tile([P, PACK, 2 * PAGES], F32, f"centre{pair}") for pair in range(CHUNKS // 2)]
+        centre = [tile([P, 2 * PAGES, PACK], F32, f"centre{pair}") for pair in range(CHUNKS // 2)]
         hv = [tile([P, CHUNK * PACK], F32, f"hv{c}") for c in range(CHUNKS)]
         hs = [tile([P, CHUNK * PACK], BF16, f"hs{c}") for c in range(CHUNKS)]
 
@@ -152,11 +151,11 @@ def tile_attend_blrcentred_asked_kernel(tc, query, query2, keys_words, keys_scal
 
         def page_centres(pair):
             for t in range(PACK):
-                nc.scalar.activation(centre[pair][:, t, :], sums[pair][:, t, :], ACT.Copy, scale=share_mean[:, t : t + 1])
+                nc.scalar.activation(centre[pair][:, :, t], sums[pair][:, t, :], ACT.Copy, scale=share_mean[:, t : t + 1])
 
         def squash(c):
             centred = tile([P, CHUNK * PACK], F32, f"centred{c}")
-            spread = centre[c // 2][:, :, own_pages(c)].rearrange("p t g -> p g t").unsqueeze(2)
+            spread = centre[c // 2][:, own_pages(c), :].unsqueeze(2)
             nc.vector.tensor_tensor(centred[:].rearrange("p (g j t) -> p g j t", j=PAGE, t=PACK),
                                     zh[c][:].rearrange("p t (g j) -> p g j t", j=PAGE),
                                     spread.broadcast_to([P, PAGES, PAGE, PACK]), ALU.subtract)
@@ -175,36 +174,32 @@ def tile_attend_blrcentred_asked_kernel(tc, query, query2, keys_words, keys_scal
         nc.vector.tensor_reduce(neg_max[:], a_scores[:], AX.X, ALU.max, negate=True)
         expo = tile([P, I], F32, "expo")
         nc.scalar.activation(expo[:], a_scores[:], ACT.Exp, bias=neg_max[:])
-        p = tile([P, I], F32, "p")
-        nc.gpsimd.tensor_tensor(p[:], expo[:], gate[:], ALU.mult)
         page_sums(0)
         page_sums(1)
         page_centres(0)
         page_sums(2)
         squash(0)
-        scale(nc.gpsimd, 0)
         page_sums(3)
         page_centres(1)
         for c in range(1, CHUNKS):
             squash(c)
         g_grouped = interleave(nc.scalar.copy, g_raw, "g_grouped")
+        p = tile([P, I], F32, "p")
         z = tile([P, 1], F32, "z")
-        nc.scalar.activation(expo[:], p[:], ACT.Copy, accum_out=z[:])
+        nc.vector.scalar_tensor_tensor(p[:], expo[:], 1.0, gate[:], ALU.mult, ALU.mult, accum_out=z[:])
         g_codes, g_plane = quantise(g_grouped[:], Q, "g")
         c0 = psum.tile([P, I], F32, name="c0")
-        scale(nc.vector, 1)
-        project(0)
-        scale(nc.vector, 2)
-        project(1)
-        scale(nc.vector, 3)
-        project(2)
+        scale(nc.vector, 0)
         rz = tile([P, 1], F32, "rz")
         nc.vector.reciprocal(rz[:], z[:])
-        project(3)
+        for c in range(1, CHUNKS):
+            scale(nc.vector, c)
+            project(c - 1)
+        project(CHUNKS - 1)
         gain = tile([P, 1], F32, "gain")
-        nc.vector.tensor_scalar(gain[:], rz[:], 512.0, None, ALU.mult)
+        nc.scalar.activation(gain[:], rz[:], ACT.Copy, scale=512.0)
         neg_rz = tile([P, 1], F32, "neg_rz")
-        nc.vector.tensor_scalar(neg_rz[:], rz[:], -1.0, None, ALU.mult)
+        nc.scalar.activation(neg_rz[:], rz[:], ACT.Copy, scale=-1.0)
 
         cp = tile([P, I], F32, "cp")
         total = tile([P, 1], F32, "total")

@@ -25,6 +25,7 @@ CHUNKS = I // CHUNK
 PAGES = CHUNK // PAGE
 HALVES = 2
 OUT_PARTS = 4
+SCALAR_CHUNK = 1
 
 
 def tile_attend_blrcentred_asked_kernel(tc, query, query2, keys_words, keys_scales, tab_words, tab_scales,
@@ -47,12 +48,13 @@ def tile_attend_blrcentred_asked_kernel(tc, query, query2, keys_words, keys_scal
         warm = tile([P, 2], F32, "warm")
         nc.vector.memset(warm[:, 0:1], 0.0)
         placed = tile([P, T], F32, "placed")
-        nc.vector.memset(placed[:], 0.0)
+        nc.vector.memset(placed[:, 0 : T // 2], 0.0)
+        for start in range(T // 2, T, 256):
+            nc.gpsimd.memset(placed[:, start : start + 256], 0.0)
 
-        def load_scale_rows(queue, window, scales, quads):
-            for quad in quads:
-                queue.dma_start(window[32 * quad : 32 * quad + 4, :].bitcast(I32),
-                                scales[0, 4 * quad : 4 * quad + 4, :].bitcast(I32))
+        def load_scale_rows(window, scales):
+            for row in range(4):
+                nc.sync.dma_start(window[row:P:32, :].bitcast(I32), scales[0, row:16:4, :].bitcast(I32))
 
         def load_rows(source, name, tag):
             rows = tile([P, PACK, source.shape[1]], F32, name, tag)
@@ -67,10 +69,10 @@ def tile_attend_blrcentred_asked_kernel(tc, query, query2, keys_words, keys_scal
         half = R // HALVES
         nc.scalar.activation(warm[:, 1:2], warm[:, 0:1], ACT.Sigmoid)
         key_pool = load_words(keys_words, "key_pool", "key_pool")
-        load_scale_rows(nc.sync, key_bytes, keys_scales, range(4))
+        load_scale_rows(key_bytes, keys_scales)
         q2_raw = load_rows(query2, "q2_raw", "q2_raw")
         w_lo = load_rows(w1[:, 0:half], "w_lo", "w_lo")
-        load_scale_rows(nc.sync, tab_bytes, tab_scales, range(4))
+        load_scale_rows(tab_bytes, tab_scales)
         tab_pool = load_words(tab_words, "tab_pool", "tab_pool")
         w_hi = load_rows(w1[:, half:R], "w_hi", "w_hi")
         q_raw = load_rows(query, "q_raw", "q_raw")
@@ -155,15 +157,29 @@ def tile_attend_blrcentred_asked_kernel(tc, query, query2, keys_words, keys_scal
 
         def squash(c):
             centred = tile([P, CHUNK * PACK], F32, f"centred{c}")
-            spread = centre[c // 2][:, own_pages(c), :].unsqueeze(2)
-            nc.vector.tensor_tensor(centred[:].rearrange("p (g j t) -> p g j t", j=PAGE, t=PACK),
-                                    zh[c][:].rearrange("p t (g j) -> p g j t", j=PAGE),
-                                    spread.broadcast_to([P, PAGES, PAGE, PACK]), ALU.subtract)
+            pages = centre[c // 2][:, own_pages(c), :]
+            if c == SCALAR_CHUNK:
+                nc.vector.tensor_tensor(centred[:].rearrange("p (t g j) -> p t g j", j=PAGE, t=PACK),
+                                        zh[c][:].rearrange("p t (g j) -> p t g j", j=PAGE),
+                                        pages.rearrange("p g t -> p t g").unsqueeze(3).broadcast_to([P, PACK, PAGES, PAGE]),
+                                        ALU.subtract)
+            else:
+                nc.vector.tensor_tensor(centred[:].rearrange("p (g j t) -> p g j t", j=PAGE, t=PACK),
+                                        zh[c][:].rearrange("p t (g j) -> p g j t", j=PAGE),
+                                        pages.unsqueeze(2).broadcast_to([P, PAGES, PAGE, PACK]), ALU.subtract)
             nc.scalar.activation(hv[c][:], centred[:], ACT.Tanh)
 
         def scale(engine, c):
             engine.tensor_tensor(hs[c][:].rearrange("p (i t) -> p i t", t=PACK), hv[c][:].rearrange("p (i t) -> p i t", t=PACK),
                                  hsc_sb[:].unsqueeze(1).broadcast_to([P, CHUNK, PACK]), ALU.mult)
+
+        def scale_by_places(c):
+            places = tile([P, PACK, CHUNK], BF16, "places")
+            for t in range(PACK):
+                nc.scalar.activation(places[:, t, :], hv[c][:, t * CHUNK : (t + 1) * CHUNK], ACT.Copy,
+                                     scale=hsc_sb[:, t : t + 1])
+            nc.scalar.copy(hs[c][:].rearrange("p (n i t) -> p n t i", i=4, t=PACK),
+                           places[:].rearrange("p t (n i) -> p n t i", i=4))
 
         def project(c):
             h_codes, h_plane = quantise(hs[c][:], CHUNK, f"hs{c}")
@@ -179,23 +195,26 @@ def tile_attend_blrcentred_asked_kernel(tc, query, query2, keys_words, keys_scal
         page_centres(0)
         page_sums(2)
         squash(0)
+        scale(nc.gpsimd, 0)
         page_sums(3)
         page_centres(1)
+        g_grouped = interleave(nc.scalar.copy, g_raw, "g_grouped")
         for c in range(1, CHUNKS):
             squash(c)
-        g_grouped = interleave(nc.scalar.copy, g_raw, "g_grouped")
+        scale_by_places(SCALAR_CHUNK)
         p = tile([P, I], F32, "p")
         z = tile([P, 1], F32, "z")
         nc.vector.scalar_tensor_tensor(p[:], expo[:], 1.0, gate[:], ALU.mult, ALU.mult, accum_out=z[:])
         g_codes, g_plane = quantise(g_grouped[:], Q, "g")
         c0 = psum.tile([P, I], F32, name="c0")
-        scale(nc.vector, 0)
+        scale(nc.vector, 2)
         rz = tile([P, 1], F32, "rz")
         nc.vector.reciprocal(rz[:], z[:])
-        for c in range(1, CHUNKS):
-            scale(nc.vector, c)
-            project(c - 1)
-        project(CHUNKS - 1)
+        project(0)
+        scale(nc.vector, 3)
+        project(2)
+        project(1)
+        project(3)
         gain = tile([P, 1], F32, "gain")
         nc.scalar.activation(gain[:], rz[:], ACT.Copy, scale=512.0)
         neg_rz = tile([P, 1], F32, "neg_rz")

@@ -24,8 +24,8 @@ CHUNK = 128
 CHUNKS = I // CHUNK
 PAGES = CHUNK // PAGE
 HALVES = 2
-OUT_PARTS = 4
-SCALAR_CHUNK = 1
+OUT_EDGES = (0, 256, 768, 1280, 1792, 2048)
+SCALAR_CHUNK = 0
 
 
 def tile_attend_blrcentred_asked_kernel(tc, query, query2, keys_words, keys_scales, tab_words, tab_scales,
@@ -48,9 +48,7 @@ def tile_attend_blrcentred_asked_kernel(tc, query, query2, keys_words, keys_scal
         warm = tile([P, 2], F32, "warm")
         nc.vector.memset(warm[:, 0:1], 0.0)
         placed = tile([P, T], F32, "placed")
-        nc.vector.memset(placed[:, 0 : T // 2], 0.0)
-        for start in range(T // 2, T, 256):
-            nc.gpsimd.memset(placed[:, start : start + 256], 0.0)
+        nc.vector.memset(placed[:], 0.0)
 
         def load_scale_rows(window, scales):
             for row in range(4):
@@ -72,8 +70,8 @@ def tile_attend_blrcentred_asked_kernel(tc, query, query2, keys_words, keys_scal
         load_scale_rows(key_bytes, keys_scales)
         q2_raw = load_rows(query2, "q2_raw", "q2_raw")
         w_lo = load_rows(w1[:, 0:half], "w_lo", "w_lo")
-        load_scale_rows(tab_bytes, tab_scales)
         tab_pool = load_words(tab_words, "tab_pool", "tab_pool")
+        load_scale_rows(tab_bytes, tab_scales)
         w_hi = load_rows(w1[:, half:R], "w_hi", "w_hi")
         q_raw = load_rows(query, "q_raw", "q_raw")
         share_sb = tile([P, PACK], F32, "share_sb")
@@ -83,7 +81,6 @@ def tile_attend_blrcentred_asked_kernel(tc, query, query2, keys_words, keys_scal
         nc.sync.dma_start(hsc_sb[:], hsc.rearrange("(p t) o -> p (t o)", t=PACK))
         old_sb = tile([P, T], F32, "old_sb")
         nc.sync.dma_start(old_sb[:], old)
-        part = T // OUT_PARTS
 
         def gather(window, dtype, name):
             picked = tile([P, I], dtype, name)
@@ -112,16 +109,16 @@ def tile_attend_blrcentred_asked_kernel(tc, query, query2, keys_words, keys_scal
         key_plane = gather(key_bytes, U8, "key_plane")
         q2_operand = quantise(q2_grouped[:], Q, "q2")
         b_scores = score(q2_operand, "b_scores")
-        tab_plane = gather(tab_bytes, U8, "tab_plane")
         tab_codes = gather(tab_pool, U16, "tab_codes")
+        tab_plane = gather(tab_bytes, U8, "tab_plane")
 
         w_grouped = tile([P, PACK * P * PACK], BF16, "w_grouped")
-        w_dealt = w_grouped[:].rearrange("p (t m j) -> p m j t", t=PACK, j=PACK)
+        w_dealt = w_grouped[:].rearrange("p (t m j) -> p m t j", t=PACK, j=PACK)
         span = half // PACK
-        nc.scalar.copy(w_dealt[:, 0:span], w_lo[:].rearrange("p j (m t) -> p m j t", t=PACK))
+        nc.scalar.copy(w_dealt[:, 0:span], w_lo[:].rearrange("p j (m t) -> p m t j", t=PACK))
         gate = tile([P, I], F32, "gate")
         nc.scalar.activation(gate[:], b_scores[:], ACT.Sigmoid)
-        nc.scalar.copy(w_dealt[:, span:P], w_hi[:].rearrange("p j (m t) -> p m j t", t=PACK))
+        nc.scalar.copy(w_dealt[:, span:P], w_hi[:].rearrange("p j (m t) -> p m t j", t=PACK))
         warm_exp = tile([P, 1], F32, "warm_exp")
         nc.scalar.activation(warm_exp[:], w_grouped[:, PACK * span : PACK * span + 1], ACT.Exp, scale=0.0, bias=gate[:, 0:1])
         a_scores = score(quantise(interleave(nc.vector.tensor_copy, q_raw, "q_grouped")[:], Q, "q"), "a_scores")
@@ -195,7 +192,6 @@ def tile_attend_blrcentred_asked_kernel(tc, query, query2, keys_words, keys_scal
         page_centres(0)
         page_sums(2)
         squash(0)
-        scale(nc.gpsimd, 0)
         page_sums(3)
         page_centres(1)
         g_grouped = interleave(nc.scalar.copy, g_raw, "g_grouped")
@@ -207,13 +203,14 @@ def tile_attend_blrcentred_asked_kernel(tc, query, query2, keys_words, keys_scal
         nc.vector.scalar_tensor_tensor(p[:], expo[:], 1.0, gate[:], ALU.mult, ALU.mult, accum_out=z[:])
         g_codes, g_plane = quantise(g_grouped[:], Q, "g")
         c0 = psum.tile([P, I], F32, name="c0")
-        scale(nc.vector, 2)
+        scale(nc.vector, 1)
         rz = tile([P, 1], F32, "rz")
         nc.vector.reciprocal(rz[:], z[:])
-        project(0)
+        scale(nc.vector, 2)
+        project(1)
         scale(nc.vector, 3)
         project(2)
-        project(1)
+        project(0)
         project(3)
         gain = tile([P, 1], F32, "gain")
         nc.scalar.activation(gain[:], rz[:], ACT.Copy, scale=512.0)
@@ -227,8 +224,8 @@ def tile_attend_blrcentred_asked_kernel(tc, query, query2, keys_words, keys_scal
         nc.vector.tensor_scalar(u[:], p[:], total[:], neg_rz[:], ALU.mult, ALU.mult)
         nc.vector.tensor_tensor(placed[:].indirect(offsets[:]), cp[:], u[:], ALU.add)
 
-        for s in range(OUT_PARTS):
-            cols = slice(s * part, (s + 1) * part)
-            res = tile([P, part], F32, f"res{s}")
+        for lo, hi in zip(OUT_EDGES, OUT_EDGES[1:]):
+            cols = slice(lo, hi)
+            res = tile([P, hi - lo], F32, f"res{lo}")
             nc.vector.tensor_tensor(res[:], placed[:, cols], old_sb[:, cols], ALU.add)
             nc.sync.dma_start(out[:, cols], res[:])

@@ -187,6 +187,13 @@ def tile_attend_blrcentred_asked_kernel(tc, query, query2, keys_words, keys_scal
         nc.vector.tensor_reduce(neg_max[:], a_scores[:], AX.X, ALU.max, negate=True)
         expo = tile([P, I], F32, "expo")
         nc.scalar.activation(expo[:], a_scores[:], ACT.Exp, bias=neg_max[:])
+        p = tile([P, I], F32, "p")
+        nc.gpsimd.tensor_tensor(p[:], expo[:], gate[:], ALU.mult)
+        folded = p
+        for width in (I // 2, I // 4, I // 8):
+            wide = folded
+            folded = tile([P, width], F32, f"folded{width}")
+            nc.gpsimd.tensor_tensor(folded[:], wide[:, 0:width], wide[:, width : 2 * width], ALU.add)
         page_sums(0)
         page_sums(1)
         page_centres(0)
@@ -198,12 +205,11 @@ def tile_attend_blrcentred_asked_kernel(tc, query, query2, keys_words, keys_scal
         for c in range(1, CHUNKS):
             squash(c)
         scale_by_places(SCALAR_CHUNK)
-        p = tile([P, I], F32, "p")
         z = tile([P, 1], F32, "z")
-        nc.vector.scalar_tensor_tensor(p[:], expo[:], 1.0, gate[:], ALU.mult, ALU.mult, accum_out=z[:])
-        g_codes, g_plane = quantise(g_grouped[:], Q, "g")
+        nc.vector.tensor_reduce(z[:], folded[:], AX.X, ALU.add)
         c0 = psum.tile([P, I], F32, name="c0")
         scale(nc.vector, 1)
+        g_codes, g_plane = quantise(g_grouped[:], Q, "g")
         rz = tile([P, 1], F32, "rz")
         nc.vector.reciprocal(rz[:], z[:])
         scale(nc.vector, 2)

from contextlib import ExitStack

import concourse.mybir as mybir

D, K, R, T, I, Q, G = 512, 512, 512, 2048, 512, 128, 32
FLOPS = 2 * I * (2 * D * Q + K * R + R * Q)

F32 = mybir.dt.float32
BF16 = mybir.dt.bfloat16
I32 = mybir.dt.int32
U32 = mybir.dt.uint32
U16 = mybir.dt.uint16
U8 = mybir.dt.uint8
FP8X4 = mybir.dt.float8_e4m3fn_x4
FP4X4 = mybir.dt.float4_e2m1fn_x4
ALU = mybir.AluOpType
ACT = mybir.ActivationFunctionType
AX = mybir.AxisListType

P = 128
PACK = 4
PAGE = I // G
CHUNK = 128
CHUNKS = I // CHUNK
PAGES = CHUNK // PAGE
HALVES = 2
OUT_EDGES = (0, 256, 768, 1280, 1792, 2048)
SCALAR_CHUNK = 0


def tile_attend_blrcentred_asked_kernel(tc, query, query2, keys_words, keys_scales, tab_words, tab_scales,
                                         w1, share, gout, hsc, old, offs, out):
    nc = tc.nc
    with ExitStack() as ctx:
        keep = ctx.enter_context(tc.tile_pool(name="keep", bufs=1))
        psum = ctx.enter_context(tc.psum_pool(name="psum", bufs=1))

        def tile(shape, dtype, name, tag=None):
            return keep.tile(shape, dtype, name=name, tag=tag or name, align_bytes=64)

        offsets = keep.tile([P, I // 16], U16, name="offsets")
        nc.sync.dma_start(offsets[:], offs)

        key_bytes = tile([P, T], U8, "key_bytes")
        tab_bytes = tile([P, T], U8, "tab_bytes")
        nc.vector.memset(key_bytes[:].bitcast(I32), 0)
        nc.vector.memset(tab_bytes[:].bitcast(I32), 0)
        warm = tile([P, 2], F32, "warm")
        nc.vector.memset(warm[:, 0:1], 0.0)
        placed = tile([P, T], F32, "placed")
        nc.vector.memset(placed[:], 0.0)

        def load_scale_rows(window, scales):
            for row in range(4):
                nc.sync.dma_start(window[row:P:32, :].bitcast(I32), scales[0, row:16:4, :].bitcast(I32))

        def load_rows(source, name, tag):
            rows = tile([P, PACK, source.shape[1]], F32, name, tag)
            nc.sync.dma_start(rows[:], source.rearrange("(p j) c -> p j c", j=PACK))
            return rows

        def load_words(source, name, tag):
            words = tile([P, T], U16, name, tag)
            nc.sync.dma_start(words[:].bitcast(I32), source[0].bitcast(I32))
            return words

        half = R // HALVES
        nc.scalar.activation(warm[:, 1:2], warm[:, 0:1], ACT.Sigmoid)
        key_pool = load_words(keys_words, "key_pool", "key_pool")
        load_scale_rows(key_bytes, keys_scales)
        q2_raw = load_rows(query2, "q2_raw", "q2_raw")
        w_lo = load_rows(w1[:, 0:half], "w_lo", "w_lo")
        tab_pool = load_words(tab_words, "tab_pool", "tab_pool")
        load_scale_rows(tab_bytes, tab_scales)
        w_hi = load_rows(w1[:, half:R], "w_hi", "w_hi")
        q_raw = load_rows(query, "q_raw", "q_raw")
        share_sb = tile([P, PACK], F32, "share_sb")
        nc.sync.dma_start(share_sb[:], share.rearrange("(p t) o -> p (t o)", t=PACK))
        g_raw = load_rows(gout, "g_raw", "g_raw")
        hsc_sb = tile([P, PACK], F32, "hsc_sb")
        nc.sync.dma_start(hsc_sb[:], hsc.rearrange("(p t) o -> p (t o)", t=PACK))
        old_sb = tile([P, T], F32, "old_sb")
        nc.sync.dma_start(old_sb[:], old)

        def gather(window, dtype, name):
            picked = tile([P, I], dtype, name)
            nc.vector.tensor_copy(picked[:], window[:].indirect(offsets[:]))
            return picked

        def quantise(grouped, columns, name):
            codes = tile([P, columns], U32, f"{name}_codes")
            plane = tile([P, columns], U8, f"{name}_plane")
            nc.vector.quantize_mx(out=codes[:].bitcast(FP8X4), scales=plane[:], in_=grouped)
            return codes, plane

        def interleave(copy, rows, name):
            grouped = tile([P, Q * PACK], BF16, name)
            copy(grouped[:].rearrange("p (c i j) -> p c j i", i=4, j=PACK), rows[:].rearrange("p j (c i) -> p c j i", i=4))
            return grouped

        def score(operand, name):
            bank = psum.tile([P, I], F32, name=name)
            nc.tensor.matmul_mx(out=bank[:], lhsT=operand[0][:].bitcast(FP8X4), lhsT_scale=operand[1][:],
                                rhs=key_codes[:].bitcast(FP4X4), rhs_scale=key_plane[:], start=True, stop=True)
            return bank

        key_codes = gather(key_pool, U16, "key_codes")
        q2_grouped = interleave(nc.scalar.copy, q2_raw, "q2_grouped")
        key_plane = gather(key_bytes, U8, "key_plane")
        q2_operand = quantise(q2_grouped[:], Q, "q2")
        b_scores = score(q2_operand, "b_scores")
        tab_codes = gather(tab_pool, U16, "tab_codes")
        tab_plane = gather(tab_bytes, U8, "tab_plane")

        w_grouped = tile([P, PACK * P * PACK], BF16, "w_grouped")
        w_dealt = w_grouped[:].rearrange("p (t m j) -> p m t j", t=PACK, j=PACK)
        span = half // PACK
        nc.scalar.copy(w_dealt[:, 0:span], w_lo[:].rearrange("p j (m t) -> p m t j", t=PACK))
        gate = tile([P, I], F32, "gate")
        nc.scalar.activation(gate[:], b_scores[:], ACT.Sigmoid)
        nc.scalar.copy(w_dealt[:, span:P], w_hi[:].rearrange("p j (m t) -> p m t j", t=PACK))
        warm_exp = tile([P, 1], F32, "warm_exp")
        nc.scalar.activation(warm_exp[:], w_grouped[:, PACK * span : PACK * span + 1], ACT.Exp, scale=0.0, bias=gate[:, 0:1])
        a_scores = score(quantise(interleave(nc.vector.tensor_copy, q_raw, "q_grouped")[:], Q, "q"), "a_scores")
        w_codes, w_plane = quantise(w_grouped[:], R, "w")

        zh = [psum.tile([P, PACK, CHUNK], F32, name=f"zh{c}") for c in range(CHUNKS)]
        for c in range(CHUNKS):
            cols = slice(c * CHUNK, (c + 1) * CHUNK)
            for t in range(PACK):
                rows = slice(t * P, (t + 1) * P)
                nc.tensor.matmul_mx(out=zh[c][:, t, :], lhsT=w_codes[:, rows].bitcast(FP8X4), lhsT_scale=w_plane[:, rows],
                                    rhs=tab_codes[:, cols].bitcast(FP4X4), rhs_scale=tab_plane[:, cols],
                                    start=True, stop=True)

        share_mean = tile([P, PACK], F32, "share_mean")
        nc.scalar.activation(share_mean[:], share_sb[:], ACT.Copy, scale=1.0 / PAGE)

        sums = [tile([P, PACK, 2 * PAGES], F32, f"sums{pair}") for pair in range(CHUNKS // 2)]
        centre = [tile([P, 2 * PAGES, PACK], F32, f"centre{pair}") for pair in range(CHUNKS // 2)]
        hv = [tile([P, CHUNK * PACK], F32, f"hv{c}") for c in range(CHUNKS)]
        hs = [tile([P, CHUNK * PACK], BF16, f"hs{c}") for c in range(CHUNKS)]

        def own_pages(c):
            return slice((c % 2) * PAGES, (c % 2 + 1) * PAGES)

        def page_sums(c):
            nc.vector.tensor_reduce(sums[c // 2][:, :, own_pages(c)], zh[c][:].rearrange("p t (g j) -> p t g j", j=PAGE),
                                    AX.X, ALU.add)

        def page_centres(pair):
            for t in range(PACK):
                nc.scalar.activation(centre[pair][:, :, t], sums[pair][:, t, :], ACT.Copy, scale=share_mean[:, t : t + 1])

        def squash(c):
            centred = tile([P, CHUNK * PACK], F32, f"centred{c}")
            pages = centre[c // 2][:, own_pages(c), :]
            if c == SCALAR_CHUNK:
                nc.vector.tensor_tensor(centred[:].rearrange("p (t g j) -> p t g j", j=PAGE, t=PACK),
                                        zh[c][:].rearrange("p t (g j) -> p t g j", j=PAGE),
                                        pages.rearrange("p g t -> p t g").unsqueeze(3).broadcast_to([P, PACK, PAGES, PAGE]),
                                        ALU.subtract)
            else:
                nc.vector.tensor_tensor(centred[:].rearrange("p (g j t) -> p g j t", j=PAGE, t=PACK),
                                        zh[c][:].rearrange("p t (g j) -> p g j t", j=PAGE),
                                        pages.unsqueeze(2).broadcast_to([P, PAGES, PAGE, PACK]), ALU.subtract)
            nc.scalar.activation(hv[c][:], centred[:], ACT.Tanh)

        def scale(engine, c):
            engine.tensor_tensor(hs[c][:].rearrange("p (i t) -> p i t", t=PACK), hv[c][:].rearrange("p (i t) -> p i t", t=PACK),
                                 hsc_sb[:].unsqueeze(1).broadcast_to([P, CHUNK, PACK]), ALU.mult)

        def scale_by_places(c):
            places = tile([P, PACK, CHUNK], BF16, "places")
            for t in range(PACK):
                nc.scalar.activation(places[:, t, :], hv[c][:, t * CHUNK : (t + 1) * CHUNK], ACT.Copy,
                                     scale=hsc_sb[:, t : t + 1])
            nc.scalar.copy(hs[c][:].rearrange("p (n i t) -> p n t i", i=4, t=PACK),
                           places[:].rearrange("p t (n i) -> p n t i", i=4))

        def project(c):
            h_codes, h_plane = quantise(hs[c][:], CHUNK, f"hs{c}")
            nc.tensor.matmul_mx(out=c0[:, c * CHUNK : (c + 1) * CHUNK], lhsT=g_codes[:].bitcast(FP8X4), lhsT_scale=g_plane[:],
                                rhs=h_codes[:].bitcast(FP8X4), rhs_scale=h_plane[:], start=True, stop=True)

        neg_max = tile([P, 1], F32, "neg_max")
        nc.vector.tensor_reduce(neg_max[:], a_scores[:], AX.X, ALU.max, negate=True)
        expo = tile([P, I], F32, "expo")
        nc.scalar.activation(expo[:], a_scores[:], ACT.Exp, bias=neg_max[:])
        p = tile([P, I], F32, "p")
        nc.gpsimd.tensor_tensor(p[:], expo[:], gate[:], ALU.mult)
        folded = p
        for width in (I // 2, I // 4, I // 8):
            wide = folded
            folded = tile([P, width], F32, f"folded{width}")
            nc.gpsimd.tensor_tensor(folded[:], wide[:, 0:width], wide[:, width : 2 * width], ALU.add)
        page_sums(0)
        page_sums(1)
        page_centres(0)
        page_sums(2)
        squash(0)
        page_sums(3)
        page_centres(1)
        g_grouped = interleave(nc.scalar.copy, g_raw, "g_grouped")
        for c in range(1, CHUNKS):
            squash(c)
        scale_by_places(SCALAR_CHUNK)
        z = tile([P, 1], F32, "z")
        nc.vector.tensor_reduce(z[:], folded[:], AX.X, ALU.add)
        c0 = psum.tile([P, I], F32, name="c0")
        scale(nc.vector, 1)
        g_codes, g_plane = quantise(g_grouped[:], Q, "g")
        rz = tile([P, 1], F32, "rz")
        nc.vector.reciprocal(rz[:], z[:])
        scale(nc.vector, 2)
        project(1)
        scale(nc.vector, 3)
        project(2)
        project(0)
        project(3)
        gain = tile([P, 1], F32, "gain")
        nc.scalar.activation(gain[:], rz[:], ACT.Copy, scale=512.0)
        neg_rz = tile([P, 1], F32, "neg_rz")
        nc.scalar.activation(neg_rz[:], rz[:], ACT.Copy, scale=-1.0)

        cp = tile([P, I], F32, "cp")
        total = tile([P, 1], F32, "total")
        nc.vector.scalar_tensor_tensor(cp[:], c0[:], gain[:], p[:], ALU.mult, ALU.mult, accum_out=total[:])
        u = tile([P, I], F32, "u")
        nc.vector.tensor_scalar(u[:], p[:], total[:], neg_rz[:], ALU.mult, ALU.mult)
        nc.vector.tensor_tensor(placed[:].indirect(offsets[:]), cp[:], u[:], ALU.add)

        for lo, hi in zip(OUT_EDGES, OUT_EDGES[1:]):
            cols = slice(lo, hi)
            res = tile([P, hi - lo], F32, f"res{lo}")
            nc.vector.tensor_tensor(res[:], placed[:, cols], old_sb[:, cols], ALU.add)
            nc.sync.dma_start(out[:, cols], res[:])
